import numpy as np
import ml_dtypes


def mxq(x, axis, fmt="e4m3"):
    dtype, down = {"e4m3": (ml_dtypes.float8_e4m3fn, 7), "e5m2": (ml_dtypes.float8_e5m2, 14)}[fmt]
    v = np.moveaxis(np.asarray(x, np.float32).astype(ml_dtypes.bfloat16).astype(np.float64), axis, -1)
    blocks = v.reshape(v.shape[:-1] + (-1, 32))
    amax = np.abs(blocks).max(-1, keepdims=True)
    byte = np.maximum(np.where(amax > 0, np.frexp(amax)[1] - 1 + 127, 0) - down, 1)
    scale = np.exp2(byte - 127.0)
    codes = (blocks / scale).astype(np.float32).astype(dtype).astype(np.float64)
    return np.moveaxis((codes * scale).reshape(v.shape), -1, axis)


WIDE = False


def mx_kscale(k, group=512):
    if not WIDE:
        return np.ones(k)
    levels = np.array([10, -10, 5, -5, 0])
    if group != 512:
        return np.exp2(np.random.permutation(np.resize(levels, k // group))).repeat(group)
    if k % 512:
        return np.exp2(np.random.permutation(np.resize(levels, k // 32))).repeat(32)
    a = np.empty((k // 512, 16))
    for p in range(k // 512):
        a[p, :8] = np.random.permutation(np.resize(levels, 8))
        for g in range(8):
            far = levels[np.abs(levels - a[p, g]) >= 10]
            a[p, g + 8] = far[np.random.randint(len(far))]
    return np.exp2(a.ravel()).repeat(32)


def f64(x):
    return np.asarray(x).astype(np.float64)


def striped(idx):
    return np.tile(np.asarray(idx).reshape(-1, 16).T, (8, 1)).astype(np.uint16)


def unstriped(offs):
    return offs[:16].T.reshape(-1).astype(np.int64)


H, KV, D, NQ, N = 8, 2, 128, 512, 512


def setup_inputs():
    n = np.random.standard_normal
    s = mx_kscale(D, 0)[:, None]
    u = mx_kscale(N)
    t = np.random.uniform(0.5, 2.0, N) * u
    v = n((KV, N, 128))
    return {
        "qT": (n((H, D, NQ)) * s * (0.70 / np.sqrt(D))).astype(np.float32),
        "kT": (n((KV, D, N)) / s).astype(np.float32),
        "t": t.reshape(N, 1).astype(np.float32),
        "v": (v / t[:, None]).astype(np.float32),
        "kb": (0.5 * n((N, 1))).astype(np.float32),
        "mask": (np.arange(N)[:, None] <= np.sort(np.random.randint(N // 4, N, NQ))[None, :]).astype(np.float32),
    }


def reference(qT, kT, t, v, kb, mask):
    a = np.repeat(mxq(f64(kT), 1, "e4m3"), H // KV, 0).transpose(0, 2, 1) @ mxq(f64(qT), 1, "e4m3")
    a = a + f64(kb)
    p = 1.0 / (1.0 + np.exp(-a))
    p = p * f64(mask)
    w = p * f64(t)
    y = mxq(w, 1, "e4m3").transpose(0, 2, 1) @ np.repeat(mxq(f64(v), 1, "e4m3"), H // KV, 0)
    y = y / 16.0
    return y

@@ -1,0 +1,252 @@
+from contextlib import ExitStack
+
+import concourse.mybir as mybir
+
+H, KV, D, NQ, N = 8, 2, 128, 512, 512
+FLOPS = 2 * 2 * H * NQ * N * D
+
+F32 = mybir.dt.float32
+BF16 = mybir.dt.bfloat16
+U32 = mybir.dt.uint32
+U8 = mybir.dt.uint8
+FP8X4 = mybir.dt.float8_e4m3fn_x4
+ACT = mybir.ActivationFunctionType
+ALU = mybir.AluOpType
+
+P = 128
+PACK = 4
+ROWS = 32
+HALF = 256
+CH = 128
+
+
+def tile_rows_a_sigmoid_kb_mask_kernel(tc, qT, kT, t, v, kb, mask, out):
+    nc = tc.nc
+    with ExitStack() as ctx:
+        keep = ctx.enter_context(tc.tile_pool(name="keep", bufs=1))
+        work = ctx.enter_context(tc.tile_pool(name="work", bufs=17))
+        psum = ctx.enter_context(tc.psum_pool(name="psum", bufs=1))
+        ctx.enter_context(tc.manual_schedule())
+
+        rounds = [(0, 0), (1, 0), (0, 1), (1, 1)]
+
+        k_raw = keep.tile([P, PACK, N], F32, name="k_raw")
+        q_raw = [keep.tile([P, PACK, HALF], F32, name="q_raw%d" % i) for i in range(4)]
+        m_raw = [keep.tile([P, PACK, HALF], F32, name="m_raw%d" % u) for u in range(2)]
+        mt = [keep.tile([P, PACK, HALF], F32, name="mt%d" % u) for u in range(2)]
+        v_raw = keep.tile([P, KV, PACK, D], F32, name="v_raw")
+        kb_sb = keep.tile([P, PACK], F32, name="kb_sb")
+        t_sb = keep.tile([P, PACK], F32, name="t_sb")
+        warm_in = keep.tile([P, 1], F32, name="warm_in")
+        warm_out = keep.tile([P, 1], F32, name="warm_out")
+
+        k16 = [keep.tile([P, 2, CH, PACK], BF16, name="k16_%d" % i, align_bytes=64) for i in range(2)]
+        k_codes = [keep.tile([P, 2 * CH], U32, name="k_codes%d" % i, align_bytes=64) for i in range(2)]
+        k_scales = [keep.tile([P, 2 * CH], U8, name="k_scales%d" % i, align_bytes=64) for i in range(2)]
+        q16 = [keep.tile([P, HALF, PACK], BF16, name="q16_%d" % i, align_bytes=64) for i in range(4)]
+        q_codes = [keep.tile([P, HALF], U32, name="q_codes%d" % i, align_bytes=64) for i in range(4)]
+        q_scales = [keep.tile([P, HALF], U8, name="q_scales%d" % i, align_bytes=64) for i in range(4)]
+        v16 = keep.tile([P, KV, D, PACK], BF16, name="v16", align_bytes=64)
+        v_codes = keep.tile([P, KV * D], U32, name="v_codes", align_bytes=64)
+        v_scales = keep.tile([P, KV * D], U8, name="v_scales", align_bytes=64)
+
+        banks = {}
+        for g in range(4):
+            for rp in range(2):
+                if g in (1, 2) and rp == 1:
+                    banks[g, rp] = banks[g, 0]
+                else:
+                    banks[g, rp] = psum.tile([P, 4 * CH], F32, name="s_bank%d_%d" % (g, rp))
+        y_banks = [psum.tile([P, 4 * CH], F32, name="y_bank%d" % i) for i in range(2)]
+
+        q_view = qT.rearrange("h (p j) n -> (h p) j n", j=PACK)
+        k_view = kT.rearrange("h (p j) n -> h p j n", j=PACK)
+        m_view = mask.rearrange("(p r) q -> p r q", r=PACK)
+
+        def load_q(i, eng_lo, eng_hi):
+            n, u = rounds[i]
+            cols = slice(HALF * u, HALF * (u + 1))
+            eng_lo.dma_start(out=q_raw[i][0:64], in_=q_view[64 * n : 64 * n + 64, :, cols])
+            eng_hi.dma_start(out=q_raw[i][64:128], in_=q_view[128 + 64 * n : 192 + 64 * n, :, cols])
+
+        def load_mask(u):
+            nc.sync.dma_start(out=m_raw[u][:], in_=m_view[:, :, HALF * u : HALF * (u + 1)])
+
+        def quantize(codes, scales, src):
+            nc.vector.quantize_mx(out=codes[:].bitcast(FP8X4), scales=scales[:], in_=src)
+
+        def cast_k(rp, copy):
+            src = k_raw[:].rearrange("p j (s r) -> p s j r", r=PACK)[:, :, :, 2 * rp : 2 * rp + 2]
+            copy(out=k16[rp][:].rearrange("p r s j -> p s j r"), in_=src)
+
+        def quant_k(rp):
+            quantize(k_codes[rp], k_scales[rp], k16[rp][:].rearrange("p r s j -> p (r s j)"))
+
+        def cast_q(i, copy):
+            copy(
+                out=q16[i][:].rearrange("p (c e) j -> p c j e", e=2),
+                in_=q_raw[i][:].rearrange("p j (c e) -> p c j e", e=2),
+            )
+
+        def quant_q(i):
+            quantize(q_codes[i], q_scales[i], q16[i][:].rearrange("p c j -> p (c j)"))
+
+        def cast_v():
+            nc.vector.tensor_copy(
+                out=v16[:].rearrange("p h (c e) j -> p h c j e", e=2),
+                in_=v_raw[:].rearrange("p h j (c e) -> p h c j e", e=2),
+            )
+
+        def quant_v():
+            quantize(v_codes, v_scales, v16[:].rearrange("p h c j -> p (h c j)"))
+
+        def make_mt(u):
+            for r in range(PACK):
+                nc.vector.tensor_scalar(
+                    out=mt[u][:, r, :], in0=m_raw[u][:, r, :], scalar1=t_sb[:, r : r + 1], scalar2=None, op0=ALU.mult
+                )
+
+        for g in range(4):
+            eng = nc.sync if g < 2 else nc.scalar
+            eng.dma_start(out=k_raw[ROWS * g : ROWS * (g + 1)], in_=k_view[g // 2])
+        load_q(0, nc.sync, nc.scalar)
+        nc.scalar.dma_start(out=kb_sb[:], in_=kb.rearrange("(p r) o -> p (r o)", r=PACK))
+        nc.sync.dma_start(out=t_sb[:], in_=t.rearrange("(p r) o -> p (r o)", r=PACK))
+        load_mask(0)
+        nc.vector.memset(warm_in[:], 0.0)
+        nc.scalar.activation(out=warm_out[:], in_=warm_in[:], func=ACT.Sigmoid)
+        load_q(1, nc.sync, nc.scalar)
+        nc.sync.dma_start(out=v_raw[:], in_=v.rearrange("h (p j) e -> p h j e", j=PACK))
+        load_q(2, nc.sync, nc.sync)
+        load_mask(1)
+        load_q(3, nc.sync, nc.sync)
+
+        cast_k(0, nc.vector.tensor_copy)
+        cast_k(1, nc.scalar.copy)
+        quant_k(0)
+        cast_q(0, nc.vector.tensor_copy)
+        quant_k(1)
+        quant_q(0)
+        make_mt(0)
+        cast_q(1, nc.vector.tensor_copy)
+
+        units = [(i, g) for i in range(4) for g in range(4)]
+        keyed = [(2 * n, i, g, 0) for n, (i, g) in enumerate(units)]
+        keyed += [(2 * n + 3 if n else 1, i, g, 1) for n, (i, g) in enumerate(units)]
+        fills = [(i, g, rp) for key, i, g, rp in sorted(keyed)]
+        bank_of = [(g, rp if g in (0, 3) else 0) for i, g, rp in fills]
+        last_user = [max([e for e in range(f) if bank_of[e] == bank_of[f]], default=-1) for f in range(len(fills))]
+        pieces = [(n, 0, 2) for n in range(len(units) - 1)] + [(len(units) - 1, 0, 1), (len(units) - 1, 1, 1)]
+        p_tiles = {}
+        w_tiles = {}
+        wq = {}
+
+        def fill(f):
+            i, g, rp = fills[f]
+            rows = slice(ROWS * g, ROWS * (g + 1))
+            for r in range(2):
+                for c in range(2):
+                    kc = slice(CH * r, CH * (r + 1))
+                    qc = slice(CH * c, CH * (c + 1))
+                    nc.tensor.matmul_mx(
+                        out=banks[g, rp][:, HALF * r + CH * c : HALF * r + CH * (c + 1)],
+                        lhsT=k_codes[rp][rows, kc].bitcast(FP8X4),
+                        lhsT_scale=k_scales[rp][rows, kc],
+                        rhs=q_codes[i][rows, qc].bitcast(FP8X4),
+                        rhs_scale=q_scales[i][rows, qc],
+                        start=True,
+                        stop=True,
+                    )
+
+        def sigmoid(f):
+            i, g, rp = fills[f]
+            if rp == 0:
+                p_tiles[i, g] = work.tile([P, PACK, HALF], F32, name="p_tile")
+            for r in range(2):
+                rr = 2 * rp + r
+                nc.scalar.activation(
+                    out=p_tiles[i, g][:, rr, :],
+                    in_=banks[g, rp][:, HALF * r : HALF * (r + 1)],
+                    func=ACT.Sigmoid,
+                    bias=kb_sb[:, rr : rr + 1],
+                )
+
+        def weigh(m):
+            n, c0, nch = pieces[m]
+            i, g = units[n]
+            u = rounds[i][1]
+            cols = slice(CH * c0, CH * (c0 + nch))
+            w_tiles[m] = work.tile([P, CH * nch, PACK], BF16, name="w16", align_bytes=64)
+            nc.vector.tensor_tensor(
+                out=w_tiles[m][:].rearrange("p (c e) r -> p c r e", e=2),
+                in0=p_tiles[i, g][:, :, cols].rearrange("p r (c e) -> p c r e", e=2),
+                in1=mt[u][:, :, cols].rearrange("p r (c e) -> p c r e", e=2),
+                op=ALU.mult,
+            )
+
+        def quant_w(m):
+            nch = pieces[m][2]
+            codes = work.tile([P, CH * nch], U32, name="w_codes", align_bytes=64)
+            scales = work.tile([P, CH * nch], U8, name="w_scales", align_bytes=64)
+            wq[m] = (codes, scales)
+            quantize(codes, scales, w_tiles[m][:].rearrange("p c r -> p (c r)"))
+
+        def finish(m):
+            n, c0, nch = pieces[m]
+            i, g = units[n]
+            s, u = rounds[i]
+            head = 4 * (g // 2) + 2 * s + g % 2
+            codes, scales = wq[m]
+            vc = slice(D * (g // 2), D * (g // 2 + 1))
+            bank = y_banks[m % 2]
+            for c in range(nch):
+                qc = slice(CH * c, CH * (c + 1))
+                nc.tensor.matmul_mx(
+                    out=bank[:, D * c : D * (c + 1)],
+                    lhsT=codes[:, qc].bitcast(FP8X4),
+                    lhsT_scale=scales[:, qc],
+                    rhs=v_codes[:, vc].bitcast(FP8X4),
+                    rhs_scale=v_scales[:, vc],
+                    start=True,
+                    stop=True,
+                )
+            res = work.tile([P, nch * D], F32, name="res")
+            nc.scalar.activation(out=res[:], in_=bank[:, 0 : nch * D], func=ACT.Copy, scale=1.0 / 16.0)
+            q0 = HALF * u + CH * c0
+            nc.sync.dma_start(
+                out=out[head, q0 : q0 + CH * nch, :].rearrange("(c s) e -> s c e", c=nch),
+                in_=res[:].rearrange("s (c e) -> s c e", c=nch),
+            )
+
+        extras = {
+            0: [lambda: quant_q(1)],
+            1: [cast_v],
+            2: [quant_v],
+            3: [lambda: cast_q(2, nc.vector.tensor_copy)],
+            4: [lambda: quant_q(2)],
+            5: [lambda: make_mt(1)],
+            8: [lambda: cast_q(3, nc.vector.tensor_copy)],
+            9: [lambda: quant_q(3)],
+        }
+        LAG = 3
+        issued = 0
+        n = 0
+        for f in range(len(fills)):
+            while issued < len(fills) and issued <= f + 2 and last_user[issued] < f:
+                fill(issued)
+                issued += 1
+            sigmoid(f)
+            if fills[f][2] == 1:
+                weigh(n)
+                for extra in extras.get(n, []):
+                    extra()
+                if n >= 1:
+                    quant_w(n - 1)
+                if n >= LAG:
+                    finish(n - LAG)
+                n += 1
+        weigh(n)
+        quant_w(n - 1)
+        quant_w(n)
+        for m in range(n - LAG, n + 1):
+            finish(m)

@@ -8,6 +8,7 @@ FLOPS = 2 * 2 * H * NQ * N * D
 F32 = mybir.dt.float32
 BF16 = mybir.dt.bfloat16
 U32 = mybir.dt.uint32
+I32 = mybir.dt.int32
 U8 = mybir.dt.uint8
 FP8X4 = mybir.dt.float8_e4m3fn_x4
 ACT = mybir.ActivationFunctionType
@@ -18,6 +19,7 @@ PACK = 4
 ROWS = 32
 HALF = 256
 CH = 128
+RUN = 4
 
 
 def tile_rows_a_sigmoid_kb_mask_kernel(tc, qT, kT, t, v, kb, mask, out):
@@ -29,6 +31,7 @@ def tile_rows_a_sigmoid_kb_mask_kernel(tc, qT, kT, t, v, kb, mask, out):
         ctx.enter_context(tc.manual_schedule())
 
         rounds = [(0, 0), (1, 0), (0, 1), (1, 1)]
+        heads = [[2, 3, 4, 5], [0, 1, 6, 7]]
 
         k_raw = keep.tile([P, PACK, N], F32, name="k_raw")
         q_raw = [keep.tile([P, PACK, HALF], F32, name="q_raw%d" % i) for i in range(4)]
@@ -40,9 +43,9 @@ def tile_rows_a_sigmoid_kb_mask_kernel(tc, qT, kT, t, v, kb, mask, out):
         warm_in = keep.tile([P, 1], F32, name="warm_in")
         warm_out = keep.tile([P, 1], F32, name="warm_out")
 
-        k16 = [keep.tile([P, 2, CH, PACK], BF16, name="k16_%d" % i, align_bytes=64) for i in range(2)]
-        k_codes = [keep.tile([P, 2 * CH], U32, name="k_codes%d" % i, align_bytes=64) for i in range(2)]
-        k_scales = [keep.tile([P, 2 * CH], U8, name="k_scales%d" % i, align_bytes=64) for i in range(2)]
+        k16 = keep.tile([P, PACK, CH, PACK], BF16, name="k16", align_bytes=64)
+        k_codes = keep.tile([P, N], I32, name="k_codes", align_bytes=64)
+        k_scales = keep.tile([P, N], U8, name="k_scales", align_bytes=64)
         q16 = [keep.tile([P, HALF, PACK], BF16, name="q16_%d" % i, align_bytes=64) for i in range(4)]
         q_codes = [keep.tile([P, HALF], U32, name="q_codes%d" % i, align_bytes=64) for i in range(4)]
         q_scales = [keep.tile([P, HALF], U8, name="q_scales%d" % i, align_bytes=64) for i in range(4)]
@@ -50,24 +53,29 @@ def tile_rows_a_sigmoid_kb_mask_kernel(tc, qT, kT, t, v, kb, mask, out):
         v_codes = keep.tile([P, KV * D], U32, name="v_codes", align_bytes=64)
         v_scales = keep.tile([P, KV * D], U8, name="v_scales", align_bytes=64)
 
+        double = (0, 2)
         banks = {}
         for g in range(4):
-            for rp in range(2):
-                if g in (1, 2) and rp == 1:
-                    banks[g, rp] = banks[g, 0]
-                else:
-                    banks[g, rp] = psum.tile([P, 4 * CH], F32, name="s_bank%d_%d" % (g, rp))
-        y_banks = [psum.tile([P, 4 * CH], F32, name="y_bank%d" % i) for i in range(2)]
+            banks[g, 0] = psum.tile([P, 4 * CH], F32, name="s_bank%d_0" % g)
+            if g in double:
+                banks[g, 1] = psum.tile([P, 4 * CH], F32, name="s_bank%d_1" % g)
+            else:
+                banks[g, 1] = banks[g, 0]
+        y_banks = [psum.tile([P, 4 * CH], F32, name="y_bank%d" % i) for i in range(4 - len(double))]
 
         q_view = qT.rearrange("h (p j) n -> (h p) j n", j=PACK)
         k_view = kT.rearrange("h (p j) n -> h p j n", j=PACK)
         m_view = mask.rearrange("(p r) q -> p r q", r=PACK)
 
-        def load_q(i, eng_lo, eng_hi):
-            n, u = rounds[i]
+        def load_q(i, part, eng):
+            s, u = rounds[i]
             cols = slice(HALF * u, HALF * (u + 1))
-            eng_lo.dma_start(out=q_raw[i][0:64], in_=q_view[64 * n : 64 * n + 64, :, cols])
-            eng_hi.dma_start(out=q_raw[i][64:128], in_=q_view[128 + 64 * n : 192 + 64 * n, :, cols])
+            if s == 0:
+                eng.dma_start(out=q_raw[i][:], in_=q_view[64:192, :, cols])
+            elif part == 0:
+                eng.dma_start(out=q_raw[i][0:64], in_=q_view[0:64, :, cols])
+            else:
+                eng.dma_start(out=q_raw[i][64:128], in_=q_view[192:256, :, cols])
 
         def load_mask(u):
             nc.sync.dma_start(out=m_raw[u][:], in_=m_view[:, :, HALF * u : HALF * (u + 1)])
@@ -76,16 +84,27 @@ def tile_rows_a_sigmoid_kb_mask_kernel(tc, qT, kT, t, v, kb, mask, out):
             nc.vector.quantize_mx(out=codes[:].bitcast(FP8X4), scales=scales[:], in_=src)
 
         def cast_k(rp, copy):
-            src = k_raw[:].rearrange("p j (s r) -> p s j r", r=PACK)[:, :, :, 2 * rp : 2 * rp + 2]
-            copy(out=k16[rp][:].rearrange("p r s j -> p s j r"), in_=src)
+            src = k_raw[0:96].rearrange("p j (s r) -> p s j r", r=PACK)[:, :, :, 2 * rp : 2 * rp + 2]
+            copy(out=k16[0:96, 2 * rp : 2 * rp + 2].rearrange("p r s j -> p s j r"), in_=src)
 
-        def quant_k(rp):
-            quantize(k_codes[rp], k_scales[rp], k16[rp][:].rearrange("p r s j -> p (r s j)"))
+        def quant_k():
+            nc.vector.quantize_mx(
+                out=k_codes[0:96].bitcast(FP8X4),
+                scales=k_scales[0:96],
+                in_=k16[0:96].rearrange("p r s j -> p (r s j)"),
+            )
+
+        def spread_k():
+            words = k_scales[:].bitcast(I32)
+            for g in (0, 2):
+                a, b = ROWS * g, ROWS * (g + 1)
+                nc.scalar.dma_start(out=k_codes[b : b + ROWS], in_=k_codes[a : a + ROWS])
+                nc.scalar.dma_start(out=words[b : b + 4], in_=words[a : a + 4])
 
         def cast_q(i, copy):
             copy(
-                out=q16[i][:].rearrange("p (c e) j -> p c j e", e=2),
-                in_=q_raw[i][:].rearrange("p j (c e) -> p c j e", e=2),
+                out=q16[i][:].rearrange("p (c e) j -> p c j e", e=RUN),
+                in_=q_raw[i][:].rearrange("p j (c e) -> p c j e", e=RUN),
             )
 
         def quant_q(i):
@@ -93,8 +112,8 @@ def tile_rows_a_sigmoid_kb_mask_kernel(tc, qT, kT, t, v, kb, mask, out):
 
         def cast_v():
             nc.vector.tensor_copy(
-                out=v16[:].rearrange("p h (c e) j -> p h c j e", e=2),
-                in_=v_raw[:].rearrange("p h j (c e) -> p h c j e", e=2),
+                out=v16[:].rearrange("p h (c e) j -> p h c j e", e=RUN),
+                in_=v_raw[:].rearrange("p h j (c e) -> p h c j e", e=RUN),
             )
 
         def quant_v():
@@ -106,37 +125,44 @@ def tile_rows_a_sigmoid_kb_mask_kernel(tc, qT, kT, t, v, kb, mask, out):
                     out=mt[u][:, r, :], in0=m_raw[u][:, r, :], scalar1=t_sb[:, r : r + 1], scalar2=None, op0=ALU.mult
                 )
 
-        for g in range(4):
-            eng = nc.sync if g < 2 else nc.scalar
-            eng.dma_start(out=k_raw[ROWS * g : ROWS * (g + 1)], in_=k_view[g // 2])
-        load_q(0, nc.sync, nc.scalar)
+        def make_mt_scalar(u):
+            for r in range(PACK):
+                nc.scalar.activation(out=mt[u][:, r, :], in_=m_raw[u][:, r, :], func=ACT.Copy, scale=t_sb[:, r : r + 1])
+
+        nc.sync.dma_start(out=k_raw[0:ROWS], in_=k_view[0])
+        nc.scalar.dma_start(out=k_raw[2 * ROWS : 3 * ROWS], in_=k_view[1])
+        load_q(0, 0, nc.sync)
         nc.scalar.dma_start(out=kb_sb[:], in_=kb.rearrange("(p r) o -> p (r o)", r=PACK))
         nc.sync.dma_start(out=t_sb[:], in_=t.rearrange("(p r) o -> p (r o)", r=PACK))
         load_mask(0)
         nc.vector.memset(warm_in[:], 0.0)
+        nc.vector.memset(k_raw[ROWS : 2 * ROWS], 0.0)
+        nc.vector.memset(k_scales[:].bitcast(I32), 0)
         nc.scalar.activation(out=warm_out[:], in_=warm_in[:], func=ACT.Sigmoid)
-        load_q(1, nc.sync, nc.scalar)
-        nc.sync.dma_start(out=v_raw[:], in_=v.rearrange("h (p j) e -> p h j e", j=PACK))
-        load_q(2, nc.sync, nc.sync)
-        load_mask(1)
-        load_q(3, nc.sync, nc.sync)
+        load_q(1, 0, nc.sync)
+        load_q(1, 1, nc.scalar)
 
         cast_k(0, nc.vector.tensor_copy)
         cast_k(1, nc.scalar.copy)
-        quant_k(0)
+        quant_k()
+        spread_k()
+        nc.sync.dma_start(out=v_raw[:], in_=v.rearrange("h (p j) e -> p h j e", j=PACK))
+        load_q(2, 0, nc.sync)
+        load_mask(1)
+        load_q(3, 0, nc.sync)
+        load_q(3, 1, nc.sync)
         cast_q(0, nc.vector.tensor_copy)
-        quant_k(1)
         quant_q(0)
         make_mt(0)
         cast_q(1, nc.vector.tensor_copy)
+        quant_q(1)
 
-        units = [(i, g) for i in range(4) for g in range(4)]
-        keyed = [(2 * n, i, g, 0) for n, (i, g) in enumerate(units)]
-        keyed += [(2 * n + 3 if n else 1, i, g, 1) for n, (i, g) in enumerate(units)]
-        fills = [(i, g, rp) for key, i, g, rp in sorted(keyed)]
-        bank_of = [(g, rp if g in (0, 3) else 0) for i, g, rp in fills]
+        fills = [(0, 0, 0), (0, 0, 1), (0, 2, 0), (0, 2, 1), (0, 1, 0), (0, 3, 0), (1, 0, 0), (0, 1, 1), (1, 2, 0), (0, 3, 1), (1, 0, 1), (1, 1, 0), (1, 2, 1), (1, 3, 0), (2, 0, 0), (1, 1, 1), (2, 2, 0), (1, 3, 1), (2, 0, 1), (2, 1, 0), (2, 2, 1), (2, 3, 0), (3, 0, 0), (2, 1, 1), (3, 2, 0), (2, 3, 1), (3, 0, 1), (3, 1, 0), (3, 2, 1), (3, 3, 0), (3, 1, 1), (3, 3, 1)]
+        units = [(i, g) for i, g, rp in fills if rp == 1]
+        bank_of = [(g, rp if g in double else 0) for i, g, rp in fills]
         last_user = [max([e for e in range(f) if bank_of[e] == bank_of[f]], default=-1) for f in range(len(fills))]
-        pieces = [(n, 0, 2) for n in range(len(units) - 1)] + [(len(units) - 1, 0, 1), (len(units) - 1, 1, 1)]
+        last = len(units) - 1
+        pieces = [(n, 0, 2) for n in range(last)] + [(last, 0, 1), (last, 1, 1)]
         p_tiles = {}
         w_tiles = {}
         wq = {}
@@ -146,12 +172,12 @@ def tile_rows_a_sigmoid_kb_mask_kernel(tc, qT, kT, t, v, kb, mask, out):
             rows = slice(ROWS * g, ROWS * (g + 1))
             for r in range(2):
                 for c in range(2):
-                    kc = slice(CH * r, CH * (r + 1))
+                    kc = slice(CH * (2 * rp + r), CH * (2 * rp + r + 1))
                     qc = slice(CH * c, CH * (c + 1))
                     nc.tensor.matmul_mx(
                         out=banks[g, rp][:, HALF * r + CH * c : HALF * r + CH * (c + 1)],
-                        lhsT=k_codes[rp][rows, kc].bitcast(FP8X4),
-                        lhsT_scale=k_scales[rp][rows, kc],
+                        lhsT=k_codes[rows, kc].bitcast(FP8X4),
+                        lhsT_scale=k_scales[rows, kc],
                         rhs=q_codes[i][rows, qc].bitcast(FP8X4),
                         rhs_scale=q_scales[i][rows, qc],
                         start=True,
@@ -178,9 +204,9 @@ def tile_rows_a_sigmoid_kb_mask_kernel(tc, qT, kT, t, v, kb, mask, out):
             cols = slice(CH * c0, CH * (c0 + nch))
             w_tiles[m] = work.tile([P, CH * nch, PACK], BF16, name="w16", align_bytes=64)
             nc.vector.tensor_tensor(
-                out=w_tiles[m][:].rearrange("p (c e) r -> p c r e", e=2),
-                in0=p_tiles[i, g][:, :, cols].rearrange("p r (c e) -> p c r e", e=2),
-                in1=mt[u][:, :, cols].rearrange("p r (c e) -> p c r e", e=2),
+                out=w_tiles[m][:].rearrange("p (c e) r -> p c r e", e=RUN),
+                in0=p_tiles[i, g][:, :, cols].rearrange("p r (c e) -> p c r e", e=RUN),
+                in1=mt[u][:, :, cols].rearrange("p r (c e) -> p c r e", e=RUN),
                 op=ALU.mult,
             )
 
@@ -191,62 +217,79 @@ def tile_rows_a_sigmoid_kb_mask_kernel(tc, qT, kT, t, v, kb, mask, out):
             wq[m] = (codes, scales)
             quantize(codes, scales, w_tiles[m][:].rearrange("p c r -> p (c r)"))
 
-        def finish(m):
-            n, c0, nch = pieces[m]
-            i, g = units[n]
-            s, u = rounds[i]
-            head = 4 * (g // 2) + 2 * s + g % 2
-            codes, scales = wq[m]
-            vc = slice(D * (g // 2), D * (g // 2 + 1))
-            bank = y_banks[m % 2]
-            for c in range(nch):
-                qc = slice(CH * c, CH * (c + 1))
-                nc.tensor.matmul_mx(
-                    out=bank[:, D * c : D * (c + 1)],
-                    lhsT=codes[:, qc].bitcast(FP8X4),
-                    lhsT_scale=scales[:, qc],
-                    rhs=v_codes[:, vc].bitcast(FP8X4),
-                    rhs_scale=v_scales[:, vc],
-                    start=True,
-                    stop=True,
-                )
-            res = work.tile([P, nch * D], F32, name="res")
-            nc.scalar.activation(out=res[:], in_=bank[:, 0 : nch * D], func=ACT.Copy, scale=1.0 / 16.0)
-            q0 = HALF * u + CH * c0
-            nc.sync.dma_start(
-                out=out[head, q0 : q0 + CH * nch, :].rearrange("(c s) e -> s c e", c=nch),
-                in_=res[:].rearrange("s (c e) -> s c e", c=nch),
-            )
+        groups = [[0, 1], [2, 3], [4, 5], [6, 7], [8, 9], [10, 11], [12, 13], [14], [15, 16]]
 
-        extras = {
-            0: [lambda: quant_q(1)],
-            1: [cast_v],
-            2: [quant_v],
-            3: [lambda: cast_q(2, nc.vector.tensor_copy)],
-            4: [lambda: quant_q(2)],
-            5: [lambda: make_mt(1)],
-            8: [lambda: cast_q(3, nc.vector.tensor_copy)],
-            9: [lambda: quant_q(3)],
-        }
-        LAG = 3
+        def product(b):
+            bank = y_banks[b % len(y_banks)]
+            col = 0
+            for m in groups[b]:
+                n, c0, nch = pieces[m]
+                g = units[n][1]
+                codes, scales = wq[m]
+                vc = slice(D * (g // 2), D * (g // 2 + 1))
+                for c in range(nch):
+                    qc = slice(CH * c, CH * (c + 1))
+                    nc.tensor.matmul_mx(
+                        out=bank[:, col : col + D],
+                        lhsT=codes[:, qc].bitcast(FP8X4),
+                        lhsT_scale=scales[:, qc],
+                        rhs=v_codes[:, vc].bitcast(FP8X4),
+                        rhs_scale=v_scales[:, vc],
+                        start=True,
+                        stop=True,
+                    )
+                    col += D
+
+        def finish(b, on_vector=False):
+            bank = y_banks[b % len(y_banks)]
+            width = D * sum(pieces[m][2] for m in groups[b])
+            res = work.tile([P, width], F32, name="res", bufs=12)
+            if on_vector:
+                nc.vector.tensor_scalar(out=res[:], in0=bank[:, 0:width], scalar1=1.0 / 16.0, scalar2=None, op0=ALU.mult)
+            else:
+                nc.scalar.activation(out=res[:], in_=bank[:, 0:width], func=ACT.Copy, scale=1.0 / 16.0)
+            col = 0
+            for m in groups[b]:
+                n, c0, nch = pieces[m]
+                i, g = units[n]
+                s, u = rounds[i]
+                q0 = HALF * u + CH * c0
+                nc.sync.dma_start(
+                    out=out[heads[s][g], q0 : q0 + CH * nch, :].rearrange("(c s) e -> s c e", c=nch),
+                    in_=res[:, col : col + D * nch].rearrange("s (c e) -> s c e", c=nch),
+                )
+                col += D * nch
+
+        extras = {0: [lambda: cast_v()], 1: [lambda: cast_q(2, nc.vector.tensor_copy), lambda: quant_v()], 2: [lambda: make_mt(1), lambda: quant_q(2)], 6: [lambda: quant_q(3)]}
+        s_extras = {11: [lambda: cast_q(3, nc.scalar.copy)]}
+        products_at = {11: [0], 17: [1], 24: [2, 3], 29: [4], 31: [5, 6]}
+        finishes_at = {20: [0], 21: [1], 26: [2], 30: [3, 4]}
         issued = 0
         n = 0
         for f in range(len(fills)):
-            while issued < len(fills) and issued <= f + 2 and last_user[issued] < f:
+            for b in products_at.get(f, []):
+                product(b)
+            while issued < len(fills) and issued <= f + 4 and last_user[issued] < f:
                 fill(issued)
                 issued += 1
             sigmoid(f)
+            for b in finishes_at.get(f, []):
+                finish(b)
+            for extra in s_extras.get(f, []):
+                extra()
             if fills[f][2] == 1:
                 weigh(n)
                 for extra in extras.get(n, []):
                     extra()
                 if n >= 1:
                     quant_w(n - 1)
-                if n >= LAG:
-                    finish(n - LAG)
                 n += 1
-        weigh(n)
-        quant_w(n - 1)
-        quant_w(n)
-        for m in range(n - LAG, n + 1):
-            finish(m)
+        weigh(last + 1)
+        quant_w(last)
+        quant_w(last + 1)
+        finish(5)
+        product(7)
+        finish(6)
+        product(8)
+        finish(7, True)
+        finish(8, True)

from contextlib import ExitStack

import concourse.mybir as mybir

H, KV, D, NQ, N = 8, 2, 128, 512, 512
FLOPS = 2 * 2 * H * NQ * N * D

F32 = mybir.dt.float32
BF16 = mybir.dt.bfloat16
U32 = mybir.dt.uint32
I32 = mybir.dt.int32
U8 = mybir.dt.uint8
FP8X4 = mybir.dt.float8_e4m3fn_x4
ACT = mybir.ActivationFunctionType
ALU = mybir.AluOpType

P = 128
PACK = 4
ROWS = 32
HALF = 256
CH = 128
RUN = 4


def tile_rows_a_sigmoid_kb_mask_kernel(tc, qT, kT, t, v, kb, mask, out):
    nc = tc.nc
    with ExitStack() as ctx:
        keep = ctx.enter_context(tc.tile_pool(name="keep", bufs=1))
        work = ctx.enter_context(tc.tile_pool(name="work", bufs=17))
        psum = ctx.enter_context(tc.psum_pool(name="psum", bufs=1))
        ctx.enter_context(tc.manual_schedule())

        rounds = [(0, 0), (1, 0), (0, 1), (1, 1)]
        heads = [[2, 3, 4, 5], [0, 1, 6, 7]]

        k_raw = keep.tile([P, PACK, N], F32, name="k_raw")
        q_raw = [keep.tile([P, PACK, HALF], F32, name="q_raw%d" % i) for i in range(4)]
        m_raw = [keep.tile([P, PACK, HALF], F32, name="m_raw%d" % u) for u in range(2)]
        mt = [keep.tile([P, PACK, HALF], F32, name="mt%d" % u) for u in range(2)]
        v_raw = keep.tile([P, KV, PACK, D], F32, name="v_raw")
        kb_sb = keep.tile([P, PACK], F32, name="kb_sb")
        t_sb = keep.tile([P, PACK], F32, name="t_sb")
        warm_in = keep.tile([P, 1], F32, name="warm_in")
        warm_out = keep.tile([P, 1], F32, name="warm_out")

        k16 = keep.tile([P, PACK, CH, PACK], BF16, name="k16", align_bytes=64)
        k_codes = keep.tile([P, N], I32, name="k_codes", align_bytes=64)
        k_scales = keep.tile([P, N], U8, name="k_scales", align_bytes=64)
        q16 = [keep.tile([P, HALF, PACK], BF16, name="q16_%d" % i, align_bytes=64) for i in range(4)]
        q_codes = [keep.tile([P, HALF], U32, name="q_codes%d" % i, align_bytes=64) for i in range(4)]
        q_scales = [keep.tile([P, HALF], U8, name="q_scales%d" % i, align_bytes=64) for i in range(4)]
        v16 = keep.tile([P, KV, D, PACK], BF16, name="v16", align_bytes=64)
        v_codes = keep.tile([P, KV * D], U32, name="v_codes", align_bytes=64)
        v_scales = keep.tile([P, KV * D], U8, name="v_scales", align_bytes=64)

        double = (0, 2)
        banks = {}
        for g in range(4):
            banks[g, 0] = psum.tile([P, 4 * CH], F32, name="s_bank%d_0" % g)
            if g in double:
                banks[g, 1] = psum.tile([P, 4 * CH], F32, name="s_bank%d_1" % g)
            else:
                banks[g, 1] = banks[g, 0]
        y_banks = [psum.tile([P, 4 * CH], F32, name="y_bank%d" % i) for i in range(4 - len(double))]

        q_view = qT.rearrange("h (p j) n -> (h p) j n", j=PACK)
        k_view = kT.rearrange("h (p j) n -> h p j n", j=PACK)
        m_view = mask.rearrange("(p r) q -> p r q", r=PACK)

        def load_q(i, part, eng):
            s, u = rounds[i]
            cols = slice(HALF * u, HALF * (u + 1))
            if s == 0:
                eng.dma_start(out=q_raw[i][:], in_=q_view[64:192, :, cols])
            elif part == 0:
                eng.dma_start(out=q_raw[i][0:64], in_=q_view[0:64, :, cols])
            else:
                eng.dma_start(out=q_raw[i][64:128], in_=q_view[192:256, :, cols])

        def load_mask(u):
            nc.sync.dma_start(out=m_raw[u][:], in_=m_view[:, :, HALF * u : HALF * (u + 1)])

        def quantize(codes, scales, src):
            nc.vector.quantize_mx(out=codes[:].bitcast(FP8X4), scales=scales[:], in_=src)

        def cast_k(rp, copy):
            src = k_raw[0:96].rearrange("p j (s r) -> p s j r", r=PACK)[:, :, :, 2 * rp : 2 * rp + 2]
            copy(out=k16[0:96, 2 * rp : 2 * rp + 2].rearrange("p r s j -> p s j r"), in_=src)

        def quant_k():
            nc.vector.quantize_mx(
                out=k_codes[0:96].bitcast(FP8X4),
                scales=k_scales[0:96],
                in_=k16[0:96].rearrange("p r s j -> p (r s j)"),
            )

        def spread_k():
            words = k_scales[:].bitcast(I32)
            for g in (0, 2):
                a, b = ROWS * g, ROWS * (g + 1)
                nc.scalar.dma_start(out=k_codes[b : b + ROWS], in_=k_codes[a : a + ROWS])
                nc.scalar.dma_start(out=words[b : b + 4], in_=words[a : a + 4])

        def cast_q(i, copy):
            copy(
                out=q16[i][:].rearrange("p (c e) j -> p c j e", e=RUN),
                in_=q_raw[i][:].rearrange("p j (c e) -> p c j e", e=RUN),
            )

        def quant_q(i):
            quantize(q_codes[i], q_scales[i], q16[i][:].rearrange("p c j -> p (c j)"))

        def cast_v():
            nc.vector.tensor_copy(
                out=v16[:].rearrange("p h (c e) j -> p h c j e", e=RUN),
                in_=v_raw[:].rearrange("p h j (c e) -> p h c j e", e=RUN),
            )

        def quant_v():
            quantize(v_codes, v_scales, v16[:].rearrange("p h c j -> p (h c j)"))

        def make_mt(u):
            for r in range(PACK):
                nc.vector.tensor_scalar(
                    out=mt[u][:, r, :], in0=m_raw[u][:, r, :], scalar1=t_sb[:, r : r + 1], scalar2=None, op0=ALU.mult
                )

        def make_mt_scalar(u):
            for r in range(PACK):
                nc.scalar.activation(out=mt[u][:, r, :], in_=m_raw[u][:, r, :], func=ACT.Copy, scale=t_sb[:, r : r + 1])

        nc.sync.dma_start(out=k_raw[0:ROWS], in_=k_view[0])
        nc.scalar.dma_start(out=k_raw[2 * ROWS : 3 * ROWS], in_=k_view[1])
        load_q(0, 0, nc.sync)
        nc.scalar.dma_start(out=kb_sb[:], in_=kb.rearrange("(p r) o -> p (r o)", r=PACK))
        nc.sync.dma_start(out=t_sb[:], in_=t.rearrange("(p r) o -> p (r o)", r=PACK))
        load_mask(0)
        nc.vector.memset(warm_in[:], 0.0)
        nc.vector.memset(k_raw[ROWS : 2 * ROWS], 0.0)
        nc.vector.memset(k_scales[:].bitcast(I32), 0)
        nc.scalar.activation(out=warm_out[:], in_=warm_in[:], func=ACT.Sigmoid)
        load_q(1, 0, nc.sync)
        load_q(1, 1, nc.scalar)

        cast_k(0, nc.vector.tensor_copy)
        cast_k(1, nc.scalar.copy)
        quant_k()
        spread_k()
        nc.sync.dma_start(out=v_raw[:], in_=v.rearrange("h (p j) e -> p h j e", j=PACK))
        load_q(2, 0, nc.sync)
        load_mask(1)
        load_q(3, 0, nc.sync)
        load_q(3, 1, nc.sync)
        cast_q(0, nc.vector.tensor_copy)
        quant_q(0)
        make_mt(0)
        cast_q(1, nc.vector.tensor_copy)
        quant_q(1)

        fills = [(0, 0, 0), (0, 0, 1), (0, 2, 0), (0, 2, 1), (0, 1, 0), (0, 3, 0), (1, 0, 0), (0, 1, 1), (1, 2, 0), (0, 3, 1), (1, 0, 1), (1, 1, 0), (1, 2, 1), (1, 3, 0), (2, 0, 0), (1, 1, 1), (2, 2, 0), (1, 3, 1), (2, 0, 1), (2, 1, 0), (2, 2, 1), (2, 3, 0), (3, 0, 0), (2, 1, 1), (3, 2, 0), (2, 3, 1), (3, 0, 1), (3, 1, 0), (3, 2, 1), (3, 3, 0), (3, 1, 1), (3, 3, 1)]
        units = [(i, g) for i, g, rp in fills if rp == 1]
        bank_of = [(g, rp if g in double else 0) for i, g, rp in fills]
        last_user = [max([e for e in range(f) if bank_of[e] == bank_of[f]], default=-1) for f in range(len(fills))]
        last = len(units) - 1
        pieces = [(n, 0, 2) for n in range(last)] + [(last, 0, 1), (last, 1, 1)]
        p_tiles = {}
        w_tiles = {}
        wq = {}

        def fill(f):
            i, g, rp = fills[f]
            rows = slice(ROWS * g, ROWS * (g + 1))
            for r in range(2):
                for c in range(2):
                    kc = slice(CH * (2 * rp + r), CH * (2 * rp + r + 1))
                    qc = slice(CH * c, CH * (c + 1))
                    nc.tensor.matmul_mx(
                        out=banks[g, rp][:, HALF * r + CH * c : HALF * r + CH * (c + 1)],
                        lhsT=k_codes[rows, kc].bitcast(FP8X4),
                        lhsT_scale=k_scales[rows, kc],
                        rhs=q_codes[i][rows, qc].bitcast(FP8X4),
                        rhs_scale=q_scales[i][rows, qc],
                        start=True,
                        stop=True,
                    )

        def sigmoid(f):
            i, g, rp = fills[f]
            if rp == 0:
                p_tiles[i, g] = work.tile([P, PACK, HALF], F32, name="p_tile")
            for r in range(2):
                rr = 2 * rp + r
                nc.scalar.activation(
                    out=p_tiles[i, g][:, rr, :],
                    in_=banks[g, rp][:, HALF * r : HALF * (r + 1)],
                    func=ACT.Sigmoid,
                    bias=kb_sb[:, rr : rr + 1],
                )

        def weigh(m):
            n, c0, nch = pieces[m]
            i, g = units[n]
            u = rounds[i][1]
            cols = slice(CH * c0, CH * (c0 + nch))
            w_tiles[m] = work.tile([P, CH * nch, PACK], BF16, name="w16", align_bytes=64)
            nc.vector.tensor_tensor(
                out=w_tiles[m][:].rearrange("p (c e) r -> p c r e", e=RUN),
                in0=p_tiles[i, g][:, :, cols].rearrange("p r (c e) -> p c r e", e=RUN),
                in1=mt[u][:, :, cols].rearrange("p r (c e) -> p c r e", e=RUN),
                op=ALU.mult,
            )

        def quant_w(m):
            nch = pieces[m][2]
            codes = work.tile([P, CH * nch], U32, name="w_codes", align_bytes=64)
            scales = work.tile([P, CH * nch], U8, name="w_scales", align_bytes=64)
            wq[m] = (codes, scales)
            quantize(codes, scales, w_tiles[m][:].rearrange("p c r -> p (c r)"))

        groups = [[0, 1], [2, 3], [4, 5], [6, 7], [8, 9], [10, 11], [12, 13], [14], [15, 16]]

        def product(b):
            bank = y_banks[b % len(y_banks)]
            col = 0
            for m in groups[b]:
                n, c0, nch = pieces[m]
                g = units[n][1]
                codes, scales = wq[m]
                vc = slice(D * (g // 2), D * (g // 2 + 1))
                for c in range(nch):
                    qc = slice(CH * c, CH * (c + 1))
                    nc.tensor.matmul_mx(
                        out=bank[:, col : col + D],
                        lhsT=codes[:, qc].bitcast(FP8X4),
                        lhsT_scale=scales[:, qc],
                        rhs=v_codes[:, vc].bitcast(FP8X4),
                        rhs_scale=v_scales[:, vc],
                        start=True,
                        stop=True,
                    )
                    col += D

        def finish(b, on_vector=False):
            bank = y_banks[b % len(y_banks)]
            width = D * sum(pieces[m][2] for m in groups[b])
            res = work.tile([P, width], F32, name="res", bufs=12)
            if on_vector:
                nc.vector.tensor_scalar(out=res[:], in0=bank[:, 0:width], scalar1=1.0 / 16.0, scalar2=None, op0=ALU.mult)
            else:
                nc.scalar.activation(out=res[:], in_=bank[:, 0:width], func=ACT.Copy, scale=1.0 / 16.0)
            col = 0
            for m in groups[b]:
                n, c0, nch = pieces[m]
                i, g = units[n]
                s, u = rounds[i]
                q0 = HALF * u + CH * c0
                nc.sync.dma_start(
                    out=out[heads[s][g], q0 : q0 + CH * nch, :].rearrange("(c s) e -> s c e", c=nch),
                    in_=res[:, col : col + D * nch].rearrange("s (c e) -> s c e", c=nch),
                )
                col += D * nch

        extras = {0: [lambda: cast_v()], 1: [lambda: cast_q(2, nc.vector.tensor_copy), lambda: quant_v()], 2: [lambda: make_mt(1), lambda: quant_q(2)], 6: [lambda: quant_q(3)]}
        s_extras = {11: [lambda: cast_q(3, nc.scalar.copy)]}
        products_at = {11: [0], 17: [1], 24: [2, 3], 29: [4], 31: [5, 6]}
        finishes_at = {20: [0], 21: [1], 26: [2], 30: [3, 4]}
        issued = 0
        n = 0
        for f in range(len(fills)):
            for b in products_at.get(f, []):
                product(b)
            while issued < len(fills) and issued <= f + 4 and last_user[issued] < f:
                fill(issued)
                issued += 1
            sigmoid(f)
            for b in finishes_at.get(f, []):
                finish(b)
            for extra in s_extras.get(f, []):
                extra()
            if fills[f][2] == 1:
                weigh(n)
                for extra in extras.get(n, []):
                    extra()
                if n >= 1:
                    quant_w(n - 1)
                n += 1
        weigh(last + 1)
        quant_w(last)
        quant_w(last + 1)
        finish(5)
        product(7)
        finish(6)
        product(8)
        finish(7, True)
        finish(8, True)
